import numpy as np
CORES = [32,40,48,56,64,72,80,88,96,104,112,120]
N = 12
F = 64
B1, B2, LR, EPS = 0.75, 0.875, 2.0, 0.001
def setup_inputs(rng):
    idle = rng.random((128, N * F)) < 0.125; ib = np.stack([idle[:, F * r:F * r + F] for r in range(N)])
    return {"gr": (rng.standard_normal((N, 128, N * F), dtype=np.float32) * ~idle), "m": (rng.standard_normal((N, 128, F), dtype=np.float32) * np.where(ib, 0.004, 1.0)).astype(np.float32), "v": np.where(ib, 2e-6 * 50 ** rng.random((N, 128, F)), (0.5 + rng.standard_normal((N, 128, F), dtype=np.float32) ** 2) * N).astype(np.float32), "w": rng.standard_normal((N, 128, F), dtype=np.float32)}
def setup_inputs_big(rng):
    d = setup_inputs(rng)
    for k in ("gr", "m", "v", "w"): d[k] = (d[k].astype(np.float32) * 1024.0).astype(d[k].dtype)
    return d
def setup_inputs_small(rng):
    d = setup_inputs(rng)
    for k in ("gr", "m", "v", "w"): d[k] = (d[k].astype(np.float32) * (1 / 1024.0)).astype(d[k].dtype)
    return d
def setup_inputs_apart(rng):
    d = setup_inputs(rng)
    f = (10.0 ** rng.permutation(np.linspace(-1.5, 1.5, N))).astype(np.float32).reshape(N, 1, 1)
    for k in ("gr", "m", "v", "w"): d[k] = (d[k].astype(np.float32) * f).astype(d[k].dtype)
    return d
def reference(gr, m, v, w):
    GR, M, V, W = gr.astype(np.float64), m.astype(np.float64), v.astype(np.float64), w.astype(np.float64)
    s = GR.sum(axis=0)
    sb = np.stack([s[:, F * r:F * r + F] for r in range(N)])
    m2 = B1 * M + (1 - B1) * sb
    v2 = B2 * V + (1 - B2) * sb ** 2
    w2 = W - LR * m2 / (np.sqrt(v2) + EPS)
    return {"y": np.broadcast_to(np.concatenate(list(w2), axis=1).astype(np.float32), (N, 128, N * F)), "mo": m2.astype(np.float32), "vo": v2.astype(np.float32)}

@@ -1,0 +1,216 @@
+from concourse.bass import DstId, RemoteDMATransfer
+from concourse.mybir import AluOpType, ActivationFunctionType
+
+F = 64
+W2 = 2 * F
+NP = 6
+
+SCRATCH = {
+    "G": ("sbuf", [128, NP * W2], "float32"),
+    "MVW": ("sbuf", [128, 3 * F], "float32"),
+    "Y": ("sbuf", [128, NP * W2], "float32"),
+    "MV": ("sbuf", [128, W2], "float32"),
+    "L": ("sbuf", [128, NP * W2], "float32"),
+    "MVA": ("sbuf", [128, 3 * F], "float32"),
+    "MVB": ("sbuf", [128, 3 * F], "float32"),
+    "P": ("sbuf", [128, W2], "float32"),
+    "PM": ("sbuf", [128, W2], "float32"),
+    "M3": ("sbuf", [128, W2], "float32"),
+    "WP": ("sbuf", [128, W2], "float32"),
+    "S": ("sbuf", [128, W2], "float32"),
+    "Q": ("sbuf", [128, W2], "float32"),
+    "V8": ("sbuf", [128, W2], "float32"),
+    "R2": ("sbuf", [128, W2], "float32"),
+    "D": ("sbuf", [128, W2], "float32"),
+    "I": ("sbuf", [128, W2], "float32"),
+    "MVO": ("sbuf", [128, W2], "float32"),
+    "WO": ("sbuf", [128, W2], "float32"),
+    "ACC": ("psum", [128, W2], "float32"),
+    "PP": ("psum", [128, W2], "float32"),
+    "T1": ("psum", [128, W2], "float32"),
+    "V7": ("psum", [128, W2], "float32"),
+    "U": ("psum", [128, W2], "float32"),
+}
+SEMAPHORES = ["ldg", "ldm", "sent", "st", "mvb", "aga", "agb",
+              "mvo", "mvm", "xc", "dv", "ac"] + ["rs%d" % j for j in range(NP)]
+
+
+def _plan(T, topo):
+    cores = list(T.cores)
+    n = len(cores)
+    chip = [topo.chip(c) for c in cores]
+    mate = [[q for q in range(n) if topo.mates(chip[r], chip[q])][0] for r in range(n)]
+    lows = sorted(set(min(r, mate[r]) for r in range(n)))
+    pair = [lows.index(min(r, mate[r])) for r in range(n)]
+    peers = [[[q for q in range(n) if pair[q] == k and (q == r or topo.same_plane(chip[q], chip[r]))][0]
+              for k in range(len(lows))] for r in range(n)]
+    helper = []
+    for r in range(n):
+        cand = [c for c in range(topo.CHIPS * topo.CORES_PER_CHIP)
+                if topo.chip(c) == chip[r] and c not in cores and topo.may_write(c, cores[mate[r]])]
+        same = [c for c in cand if topo.die(c) == topo.die(cores[r])]
+        helper.append((same or cand)[0])
+    return cores, mate, lows, pair, peers, helper
+
+
+def _engines(topo, src, dsts):
+    m = -1
+    for d in dsts:
+        m &= topo.mask(src, d)
+    return [b for b in range(m.bit_length()) if (m >> b) & 1]
+
+
+def _bits(eng):
+    m = 0
+    for b in eng:
+        m |= 1 << b
+    return m
+
+
+def _dst(topo, c):
+    rid, pid, _ = topo.addr(c)
+    return DstId(rid=rid, pnc=pid)
+
+
+def _rank_core(g, r, T, topo, plan):
+    cores, mate, lows, pair, peers, helper = plan
+    sem = T.sem
+    k = pair[r]
+    me = cores[r]
+    hs = [helper[peers[r][kk]] for kk in range(NP)]
+    eng = _engines(topo, me, hs)
+    ne = len(eng)
+
+    g.scalar.dma_start(T.MVW[:, 0:F], T.m[:]).then_inc(sem.ldm, 16)
+    g.scalar.dma_start(T.MVW[:, F:2 * F], T.v[:]).then_inc(sem.ldm, 16)
+    g.scalar.dma_start(T.MVW[:, 2 * F:3 * F], T.w[:]).then_inc(sem.ldm, 16)
+    g.sync.dma_start(T.G[:], T.gr[:]).then_inc(sem.ldg, 16)
+
+    rid, pid, _ = topo.addr(hs[k])
+    g.wait_ge(sem.ldm, 48)
+    g.remote_dma(out_ap=T.MVA[:], in_ap=T.MVW[:], remote_sem=sem.mvo, local_sem=sem.sent,
+                 pid=pid, routing_id=rid, dma_engine_mask=_bits(eng))
+    sent = ne
+
+    def piece(d, engs):
+        kk = (k + d) % NP
+        return RemoteDMATransfer(dst_ids=[_dst(topo, hs[kk])], dma_engine_mask=_bits(engs),
+                                 remote_sem=sem["rs%d" % k],
+                                 src=T.G[:, F * lows[kk]:F * lows[kk] + W2], dst=T.L[:, W2 * k:W2 * k + W2])
+
+    g.wait_ge(sem.ldg, 16)
+    q = ne // 4
+    g.remote_dma_fused([piece(d, eng[q * (d - 1):q * d]) for d in (1, 2, 3, 4)], local_sem=sem.sent)
+    h = ne // 2
+    g.remote_dma_fused([piece(5, eng[0:h]), piece(0, eng[h:2 * h])], local_sem=sem.sent)
+    sent += 4 * q + 2 * h
+
+    half = NP // 2 * W2
+    g.sync.wait_ge(sem.mvb, ne)
+    g.sync.dma_start(T.mo[:], T.MV[:, 0:F]).then_inc(sem.st, 16)
+    g.scalar.wait_ge(sem.mvb, ne)
+    g.scalar.dma_start(T.vo[:], T.MV[:, F:W2]).then_inc(sem.st, 16)
+    g.sync.wait_ge(sem.aga, NP // 2 * ne)
+    g.sync.dma_start(T.y[:, 0:half], T.Y[:, 0:half]).then_inc(sem.st, 16)
+    g.scalar.wait_ge(sem.agb, NP // 2 * ne)
+    g.scalar.dma_start(T.y[:, half:2 * half], T.Y[:, half:2 * half]).then_inc(sem.st, 16)
+    g.wait_ge(sem.sent, sent)
+    g.wait_ge(sem.st, 64)
+
+
+def _helper_core(g, r, T, topo, plan):
+    cores, mate, lows, pair, peers, helper = plan
+    sem = T.sem
+    V, A = g.vector, g.scalar
+    k = pair[r]
+    me = helper[r]
+    hm = helper[mate[r]]
+    ranks = [cores[peers[r][kk]] for kk in range(NP)]
+    eng = _engines(topo, me, ranks + [hm])
+    ne = len(eng)
+    allm = _bits(eng)
+    own = slice(0, F) if r < mate[r] else slice(F, W2)
+    oth = slice(F, W2) if r < mate[r] else slice(0, F)
+    add, sub, mul = AluOpType.add, AluOpType.subtract, AluOpType.mult
+
+    n = [0]
+
+    def vec(call, *a):
+        if n[0]:
+            V.wait_ge(sem.dv, n[0])
+        call(*a).then_inc(sem.dv, 1)
+        n[0] += 1
+        return n[0]
+
+    def prep(buf, cols):
+        vec(V.tensor_scalar, T.M3[:, cols], buf[:, 0:F], 3.0, None, mul)
+        vec(V.tensor_scalar, T.V7[:, cols], buf[:, F:2 * F], 7.0, None, mul)
+        vec(V.tensor_copy, T.WP[:, cols], buf[:, 2 * F:3 * F])
+
+    def slot(j):
+        return T.L[:, W2 * j:W2 * j + W2]
+
+    V.wait_ge(sem.mvo, ne)
+    prep(T.MVA, own)
+    order = [(k - d) % NP for d in (1, 2, 3, 4, 5, 0)]
+    count = [ne // 4] * 4 + [ne // 2] * 2
+    for j, c in zip(order[:2], count[:2]):
+        V.wait_ge(sem["rs%d" % j], c)
+    vec(V.tensor_tensor, T.ACC[:], slot(order[0]), slot(order[1]), add)
+    for j, c in zip(order[2:5], count[2:5]):
+        V.wait_ge(sem["rs%d" % j], c)
+        vec(V.tensor_tensor, T.ACC[:], T.ACC[:], slot(j), add)
+    V.wait_ge(sem["rs%d" % order[5]], count[5])
+    n_p = vec(V.tensor_tensor, T.P[:], T.ACC[:], slot(order[5]), add)
+    vec(V.tensor_copy, T.PP[:], T.P[:])
+    V.wait_ge(sem.mvm, ne)
+    prep(T.MVB, oth)
+    vec(V.tensor_tensor, T.T1[:], T.P[:], T.M3[:], add)
+    V.wait_ge(sem.xc, ne)
+    n_s = vec(V.tensor_tensor, T.S[:], T.PP[:], T.PM[:], add)
+    vec(V.tensor_tensor, T.T1[:], T.T1[:], T.PM[:], add)
+    V.wait_ge(sem.ac, 1)
+    n_v8 = vec(V.tensor_tensor, T.V8[:], T.V7[:], T.Q[:], add)
+    vec(V.tensor_scalar, T.MVO[:, 0:F], T.T1[:, own], 0.25, None, mul)
+    n_mv = vec(V.tensor_scalar, T.MVO[:, F:W2], T.V8[:, own], 0.125, None, mul)
+    V.wait_ge(sem.ac, 2)
+    vec(V.tensor_scalar, T.D[:], T.R2[:], 0.002, None, add)
+    vec(V.reciprocal, T.I[:], T.D[:])
+    vec(V.tensor_tensor, T.U[:], T.T1[:], T.I[:], mul)
+    n_w = vec(V.tensor_tensor, T.WO[:], T.WP[:], T.U[:], sub)
+
+    A.wait_ge(sem.dv, n_s)
+    A.activation(T.Q[:], T.S[:], ActivationFunctionType.Square).then_inc(sem.ac, 1)
+    A.wait_ge(sem.dv, n_v8)
+    A.activation(T.R2[:], T.V8[:], ActivationFunctionType.Sqrt, scale=0.5).then_inc(sem.ac, 1)
+
+    rid, pid, _ = topo.addr(hm)
+    g.wait_ge(sem.mvo, ne)
+    g.remote_dma(out_ap=T.MVB[:], in_ap=T.MVA[:], remote_sem=sem.mvm, local_sem=sem.sent,
+                 pid=pid, routing_id=rid, dma_engine_mask=allm)
+    g.wait_ge(sem.dv, n_p)
+    g.remote_dma(out_ap=T.PM[:], in_ap=T.P[:], remote_sem=sem.xc, local_sem=sem.sent,
+                 pid=pid, routing_id=rid, dma_engine_mask=allm)
+    rid, pid, _ = topo.addr(cores[r])
+    g.wait_ge(sem.dv, n_mv)
+    g.remote_dma(out_ap=T.MV[:], in_ap=T.MVO[:], remote_sem=sem.mvb, local_sem=sem.sent,
+                 pid=pid, routing_id=rid, dma_engine_mask=allm)
+    h3 = NP // 2
+    grp = k // h3
+    seq = [grp * h3 + (k + 1 + i) % h3 for i in range(h3)] + [(1 - grp) * h3 + (k + i) % h3 for i in range(h3)]
+    g.wait_ge(sem.dv, n_w)
+    g.remote_dma_fused([RemoteDMATransfer(dst_ids=[_dst(topo, ranks[j]) for j in seq], dma_engine_mask=allm,
+                                          remote_sem=sem.aga if grp == 0 else sem.agb,
+                                          srcs=[T.WO[:]],
+                                          dsts=[T.Y[:, F * lows[k]:F * lows[k] + W2] for j in seq])],
+                       local_sem=sem.sent)
+    g.wait_ge(sem.sent, 4 * ne)
+
+
+def rank_program(g, core, T, topo):
+    plan = _plan(T, topo)
+    r = T.rank_of(core)
+    if r is not None:
+        _rank_core(g, r, T, topo, plan)
+    elif core in plan[5]:
+        _helper_core(g, plan[5].index(core), T, topo, plan)

@@ -5,6 +5,12 @@ F = 64
 W2 = 2 * F
 NP = 6
 
+D_A = (5, 1)
+D_B = (4, 2, 3)
+G_FIRST = (0, 5, 4)
+G_SECOND = (1, 2)
+G_THIRD = (3,)
+
 SCRATCH = {
     "G": ("sbuf", [128, NP * W2], "float32"),
     "MVW": ("sbuf", [128, 3 * F], "float32"),
@@ -31,8 +37,8 @@ SCRATCH = {
     "V7": ("psum", [128, W2], "float32"),
     "U": ("psum", [128, W2], "float32"),
 }
-SEMAPHORES = ["ldg", "ldm", "sent", "st", "mvb", "aga", "agb",
-              "mvo", "mvm", "xc", "dv", "ac"] + ["rs%d" % j for j in range(NP)]
+SEMAPHORES = (["lda", "ldb", "ldm", "sent", "st", "mvb", "mvo", "mvm", "xc", "dv", "ac"]
+              + ["rs%d" % j for j in range(NP)] + ["ag%d" % j for j in range(NP)])
 
 
 def _plan(T, topo):
@@ -44,13 +50,17 @@ def _plan(T, topo):
     pair = [lows.index(min(r, mate[r])) for r in range(n)]
     peers = [[[q for q in range(n) if pair[q] == k and (q == r or topo.same_plane(chip[q], chip[r]))][0]
               for k in range(len(lows))] for r in range(n)]
-    helper = []
+    ha, hb = [], []
     for r in range(n):
         cand = [c for c in range(topo.CHIPS * topo.CORES_PER_CHIP)
                 if topo.chip(c) == chip[r] and c not in cores and topo.may_write(c, cores[mate[r]])]
         same = [c for c in cand if topo.die(c) == topo.die(cores[r])]
-        helper.append((same or cand)[0])
-    return cores, mate, lows, pair, peers, helper
+        a = (same or cand)[0]
+        rest = [c for c in cand if c != a]
+        far = [c for c in rest if topo.die(c) != topo.die(cores[r])]
+        ha.append(a)
+        hb.append((far or rest)[0])
+    return cores, mate, lows, pair, peers, ha, hb
 
 
 def _engines(topo, src, dsts):
@@ -72,63 +82,92 @@ def _dst(topo, c):
     return DstId(rid=rid, pnc=pid)
 
 
+def _runs(starts, width):
+    out = []
+    for s in sorted(starts):
+        if out and out[-1][1] == s:
+            out[-1][1] = s + width
+        else:
+            out.append([s, s + width])
+    return out
+
+
 def _rank_core(g, r, T, topo, plan):
-    cores, mate, lows, pair, peers, helper = plan
+    cores, mate, lows, pair, peers, ha, hb = plan
     sem = T.sem
     k = pair[r]
     me = cores[r]
-    hs = [helper[peers[r][kk]] for kk in range(NP)]
+    hs = [ha[peers[r][kk]] for kk in range(NP)]
     eng = _engines(topo, me, hs)
+    wide = _engines(topo, me, [ha[r], hb[r]])
+    home = [e for e in wide if e not in eng]
     ne = len(eng)
 
-    g.scalar.dma_start(T.MVW[:, 0:F], T.m[:]).then_inc(sem.ldm, 16)
-    g.scalar.dma_start(T.MVW[:, F:2 * F], T.v[:]).then_inc(sem.ldm, 16)
-    g.scalar.dma_start(T.MVW[:, 2 * F:3 * F], T.w[:]).then_inc(sem.ldm, 16)
-    g.sync.dma_start(T.G[:], T.gr[:]).then_inc(sem.ldg, 16)
+    def col(kk):
+        return F * lows[kk % NP]
 
-    rid, pid, _ = topo.addr(hs[k])
+    g.sync.dma_start(T.MVW[:, 0:F], T.m[:]).then_inc(sem.ldm, 16)
+    g.scalar.dma_start(T.MVW[:, F:2 * F], T.v[:]).then_inc(sem.ldm, 16)
+    g.sync.dma_start(T.MVW[:, 2 * F:3 * F], T.w[:]).then_inc(sem.ldm, 16)
+    ra = _runs([col(k + d) for d in (1, 2, 3, 4)], W2)
+    rb = _runs([col(k + d) for d in (5, 0)], W2)
+    for a, b in ra:
+        g.sync.dma_start(T.G[:, a:b], T.gr[:, a:b]).then_inc(sem.lda, 16)
+    for a, b in rb:
+        g.sync.dma_start(T.G[:, a:b], T.gr[:, a:b]).then_inc(sem.ldb, 16)
+
     g.wait_ge(sem.ldm, 48)
-    g.remote_dma(out_ap=T.MVA[:], in_ap=T.MVW[:], remote_sem=sem.mvo, local_sem=sem.sent,
-                 pid=pid, routing_id=rid, dma_engine_mask=_bits(eng))
-    sent = ne
+    g.remote_dma_fused([RemoteDMATransfer(dst_ids=[_dst(topo, ha[r]), _dst(topo, hb[r])], dma_engine_mask=_bits(wide),
+                                          remote_sem=sem.mvo, srcs=[T.MVW[:]], dsts=[T.MVA[:], T.MVA[:]])],
+                       local_sem=sem.sent)
+    sent = len(wide)
 
     def piece(d, engs):
         kk = (k + d) % NP
         return RemoteDMATransfer(dst_ids=[_dst(topo, hs[kk])], dma_engine_mask=_bits(engs),
                                  remote_sem=sem["rs%d" % k],
-                                 src=T.G[:, F * lows[kk]:F * lows[kk] + W2], dst=T.L[:, W2 * k:W2 * k + W2])
+                                 src=T.G[:, col(kk):col(kk) + W2], dst=T.L[:, W2 * k:W2 * k + W2])
 
-    g.wait_ge(sem.ldg, 16)
     q = ne // 4
+    g.wait_ge(sem.lda, 16 * len(ra))
     g.remote_dma_fused([piece(d, eng[q * (d - 1):q * d]) for d in (1, 2, 3, 4)], local_sem=sem.sent)
-    h = ne // 2
-    g.remote_dma_fused([piece(5, eng[0:h]), piece(0, eng[h:2 * h])], local_sem=sem.sent)
-    sent += 4 * q + 2 * h
+    g.wait_ge(sem.ldb, 16 * len(rb))
+    g.remote_dma_fused([piece(5, eng), piece(0, home)], local_sem=sem.sent)
+    sent += 4 * q + ne + len(home)
 
-    half = NP // 2 * W2
-    g.sync.wait_ge(sem.mvb, ne)
+    stores = [0]
+
+    def put(queue, ds):
+        for d in ds:
+            queue.wait_ge(sem["ag%d" % ((k - d) % NP)], len(home) if d == 0 else ne)
+        for a, b in _runs([col(k - d) for d in ds], W2):
+            queue.dma_start(T.y[:, a:b], T.Y[:, a:b]).then_inc(sem.st, 16)
+            stores[0] += 1
+
+    g.sync.wait_ge(sem.mvb, len(home))
     g.sync.dma_start(T.mo[:], T.MV[:, 0:F]).then_inc(sem.st, 16)
-    g.scalar.wait_ge(sem.mvb, ne)
+    g.scalar.wait_ge(sem.mvb, len(home))
     g.scalar.dma_start(T.vo[:], T.MV[:, F:W2]).then_inc(sem.st, 16)
-    g.sync.wait_ge(sem.aga, NP // 2 * ne)
-    g.sync.dma_start(T.y[:, 0:half], T.Y[:, 0:half]).then_inc(sem.st, 16)
-    g.scalar.wait_ge(sem.agb, NP // 2 * ne)
-    g.scalar.dma_start(T.y[:, half:2 * half], T.Y[:, half:2 * half]).then_inc(sem.st, 16)
+    put(g.sync, G_FIRST)
+    put(g.scalar, G_SECOND)
+    put(g.sync, G_THIRD)
     g.wait_ge(sem.sent, sent)
-    g.wait_ge(sem.st, 64)
+    g.wait_ge(sem.st, 16 * (2 + stores[0]))
 
 
-def _helper_core(g, r, T, topo, plan):
-    cores, mate, lows, pair, peers, helper = plan
+def _helper_core(g, r, first, T, topo, plan):
+    cores, mate, lows, pair, peers, ha, hb = plan
     sem = T.sem
     V, A = g.vector, g.scalar
     k = pair[r]
-    me = helper[r]
-    hm = helper[mate[r]]
+    me = ha[r] if first else hb[r]
+    twin = ha[mate[r]] if first else hb[mate[r]]
     ranks = [cores[peers[r][kk]] for kk in range(NP)]
-    eng = _engines(topo, me, ranks + [hm])
+    eng = _engines(topo, me, ranks + [ha[mate[r]], hb[mate[r]]])
+    home = [e for e in _engines(topo, me, [cores[r]]) if e not in eng]
     ne = len(eng)
-    allm = _bits(eng)
+    n_in = len(_engines(topo, cores[r], [ha[r], hb[r]]))
+    offm, homem = _bits(eng), _bits(home)
     own = slice(0, F) if r < mate[r] else slice(F, W2)
     oth = slice(F, W2) if r < mate[r] else slice(0, F)
     add, sub, mul = AluOpType.add, AluOpType.subtract, AluOpType.mult
@@ -142,37 +181,49 @@ def _helper_core(g, r, T, topo, plan):
         n[0] += 1
         return n[0]
 
+    m3 = T.M3 if first else T.T1
+
     def prep(buf, cols):
-        vec(V.tensor_scalar, T.M3[:, cols], buf[:, 0:F], 3.0, None, mul)
+        vec(V.tensor_scalar, m3[:, cols], buf[:, 0:F], 3.0, None, mul)
         vec(V.tensor_scalar, T.V7[:, cols], buf[:, F:2 * F], 7.0, None, mul)
         vec(V.tensor_copy, T.WP[:, cols], buf[:, 2 * F:3 * F])
 
     def slot(j):
         return T.L[:, W2 * j:W2 * j + W2]
 
-    V.wait_ge(sem.mvo, ne)
+    V.wait_ge(sem.mvo, n_in)
     prep(T.MVA, own)
-    order = [(k - d) % NP for d in (1, 2, 3, 4, 5, 0)]
-    count = [ne // 4] * 4 + [ne // 2] * 2
-    for j, c in zip(order[:2], count[:2]):
-        V.wait_ge(sem["rs%d" % j], c)
-    vec(V.tensor_tensor, T.ACC[:], slot(order[0]), slot(order[1]), add)
-    for j, c in zip(order[2:5], count[2:5]):
-        V.wait_ge(sem["rs%d" % j], c)
-        vec(V.tensor_tensor, T.ACC[:], T.ACC[:], slot(j), add)
-    V.wait_ge(sem["rs%d" % order[5]], count[5])
-    n_p = vec(V.tensor_tensor, T.P[:], T.ACC[:], slot(order[5]), add)
-    vec(V.tensor_copy, T.PP[:], T.P[:])
-    V.wait_ge(sem.mvm, ne)
-    prep(T.MVB, oth)
-    vec(V.tensor_tensor, T.T1[:], T.P[:], T.M3[:], add)
-    V.wait_ge(sem.xc, ne)
-    n_s = vec(V.tensor_tensor, T.S[:], T.PP[:], T.PM[:], add)
-    vec(V.tensor_tensor, T.T1[:], T.T1[:], T.PM[:], add)
+    n_p = 0
+    if first:
+        order = [(k - d) % NP for d in (0, 1, 2, 3, 4, 5)]
+        count = [len(home)] + [ne // 4] * 4 + [ne]
+        for j, c in zip(order[:2], count[:2]):
+            V.wait_ge(sem["rs%d" % j], c)
+        vec(V.tensor_tensor, T.ACC[:], slot(order[0]), slot(order[1]), add)
+        for j, c in zip(order[2:5], count[2:5]):
+            V.wait_ge(sem["rs%d" % j], c)
+            vec(V.tensor_tensor, T.ACC[:], T.ACC[:], slot(j), add)
+        V.wait_ge(sem["rs%d" % order[5]], count[5])
+        n_p = vec(V.tensor_tensor, T.P[:], T.ACC[:], slot(order[5]), add)
+        vec(V.tensor_copy, T.PP[:], T.P[:])
+        V.wait_ge(sem.mvm, ne)
+        prep(T.MVB, oth)
+        vec(V.tensor_tensor, T.T1[:], T.P[:], T.M3[:], add)
+        V.wait_ge(sem.xc, ne)
+        n_s = vec(V.tensor_tensor, T.S[:], T.PP[:], T.PM[:], add)
+        vec(V.tensor_tensor, T.T1[:], T.T1[:], T.PM[:], add)
+    else:
+        V.wait_ge(sem.mvm, ne)
+        prep(T.MVB, oth)
+        V.wait_ge(sem.xc, 2 * ne)
+        n_s = vec(V.tensor_tensor, T.S[:], T.P[:], T.PM[:], add)
+        vec(V.tensor_tensor, T.T1[:], T.T1[:], T.S[:], add)
     V.wait_ge(sem.ac, 1)
     n_v8 = vec(V.tensor_tensor, T.V8[:], T.V7[:], T.Q[:], add)
-    vec(V.tensor_scalar, T.MVO[:, 0:F], T.T1[:, own], 0.25, None, mul)
-    n_mv = vec(V.tensor_scalar, T.MVO[:, F:W2], T.V8[:, own], 0.125, None, mul)
+    n_mv = 0
+    if first:
+        vec(V.tensor_scalar, T.MVO[:, 0:F], T.T1[:, own], 0.25, None, mul)
+        n_mv = vec(V.tensor_scalar, T.MVO[:, F:W2], T.V8[:, own], 0.125, None, mul)
     V.wait_ge(sem.ac, 2)
     vec(V.tensor_scalar, T.D[:], T.R2[:], 0.002, None, add)
     vec(V.reciprocal, T.I[:], T.D[:])
@@ -184,27 +235,34 @@ def _helper_core(g, r, T, topo, plan):
     A.wait_ge(sem.dv, n_v8)
     A.activation(T.R2[:], T.V8[:], ActivationFunctionType.Sqrt, scale=0.5).then_inc(sem.ac, 1)
 
-    rid, pid, _ = topo.addr(hm)
-    g.wait_ge(sem.mvo, ne)
+    ycols = T.Y[:, F * lows[k]:F * lows[k] + W2]
+
+    def cast(ds, mask):
+        return RemoteDMATransfer(dst_ids=[_dst(topo, ranks[(k + d) % NP]) for d in ds], dma_engine_mask=mask,
+                                 remote_sem=sem["ag%d" % k], srcs=[T.WO[:]], dsts=[ycols for d in ds])
+
+    rid, pid, _ = topo.addr(twin)
+    g.wait_ge(sem.mvo, n_in)
     g.remote_dma(out_ap=T.MVB[:], in_ap=T.MVA[:], remote_sem=sem.mvm, local_sem=sem.sent,
-                 pid=pid, routing_id=rid, dma_engine_mask=allm)
-    g.wait_ge(sem.dv, n_p)
-    g.remote_dma(out_ap=T.PM[:], in_ap=T.P[:], remote_sem=sem.xc, local_sem=sem.sent,
-                 pid=pid, routing_id=rid, dma_engine_mask=allm)
-    rid, pid, _ = topo.addr(cores[r])
-    g.wait_ge(sem.dv, n_mv)
-    g.remote_dma(out_ap=T.MV[:], in_ap=T.MVO[:], remote_sem=sem.mvb, local_sem=sem.sent,
-                 pid=pid, routing_id=rid, dma_engine_mask=allm)
-    h3 = NP // 2
-    grp = k // h3
-    seq = [grp * h3 + (k + 1 + i) % h3 for i in range(h3)] + [(1 - grp) * h3 + (k + i) % h3 for i in range(h3)]
-    g.wait_ge(sem.dv, n_w)
-    g.remote_dma_fused([RemoteDMATransfer(dst_ids=[_dst(topo, ranks[j]) for j in seq], dma_engine_mask=allm,
-                                          remote_sem=sem.aga if grp == 0 else sem.agb,
-                                          srcs=[T.WO[:]],
-                                          dsts=[T.Y[:, F * lows[k]:F * lows[k] + W2] for j in seq])],
-                       local_sem=sem.sent)
-    g.wait_ge(sem.sent, 4 * ne)
+                 pid=pid, routing_id=rid, dma_engine_mask=offm)
+    sent = ne
+    if first:
+        g.wait_ge(sem.dv, n_p)
+        g.remote_dma_fused([RemoteDMATransfer(dst_ids=[_dst(topo, hb[mate[r]]), _dst(topo, hb[r]), _dst(topo, ha[mate[r]])],
+                                              dma_engine_mask=offm, remote_sem=sem.xc,
+                                              srcs=[T.P[:]], dsts=[T.PM[:], T.P[:], T.PM[:]])], local_sem=sem.sent)
+        rid, pid, _ = topo.addr(cores[r])
+        g.wait_ge(sem.dv, n_mv)
+        g.remote_dma(out_ap=T.MV[:], in_ap=T.MVO[:], remote_sem=sem.mvb, local_sem=sem.sent,
+                     pid=pid, routing_id=rid, dma_engine_mask=homem)
+        g.wait_ge(sem.dv, n_w)
+        g.remote_dma_fused([cast(D_A, offm), cast((0,), homem)], local_sem=sem.sent)
+        sent += ne + len(home) + ne + len(home)
+    else:
+        g.wait_ge(sem.dv, n_w)
+        g.remote_dma_fused([cast(D_B, offm)], local_sem=sem.sent)
+        sent += ne
+    g.wait_ge(sem.sent, sent)
 
 
 def rank_program(g, core, T, topo):
@@ -213,4 +271,6 @@ def rank_program(g, core, T, topo):
     if r is not None:
         _rank_core(g, r, T, topo, plan)
     elif core in plan[5]:
-        _helper_core(g, plan[5].index(core), T, topo, plan)
+        _helper_core(g, plan[5].index(core), True, T, topo, plan)
+    elif core in plan[6]:
+        _helper_core(g, plan[6].index(core), False, T, topo, plan)

from concourse.bass import DstId, RemoteDMATransfer
from concourse.mybir import AluOpType, ActivationFunctionType

F = 64
W2 = 2 * F
NP = 6

D_A = (5, 1)
D_B = (4, 2, 3)
G_FIRST = (0, 5, 4)
G_SECOND = (1, 2)
G_THIRD = (3,)

SCRATCH = {
    "G": ("sbuf", [128, NP * W2], "float32"),
    "MVW": ("sbuf", [128, 3 * F], "float32"),
    "Y": ("sbuf", [128, NP * W2], "float32"),
    "MV": ("sbuf", [128, W2], "float32"),
    "L": ("sbuf", [128, NP * W2], "float32"),
    "MVA": ("sbuf", [128, 3 * F], "float32"),
    "MVB": ("sbuf", [128, 3 * F], "float32"),
    "P": ("sbuf", [128, W2], "float32"),
    "PM": ("sbuf", [128, W2], "float32"),
    "M3": ("sbuf", [128, W2], "float32"),
    "WP": ("sbuf", [128, W2], "float32"),
    "S": ("sbuf", [128, W2], "float32"),
    "Q": ("sbuf", [128, W2], "float32"),
    "V8": ("sbuf", [128, W2], "float32"),
    "R2": ("sbuf", [128, W2], "float32"),
    "D": ("sbuf", [128, W2], "float32"),
    "I": ("sbuf", [128, W2], "float32"),
    "MVO": ("sbuf", [128, W2], "float32"),
    "WO": ("sbuf", [128, W2], "float32"),
    "ACC": ("psum", [128, W2], "float32"),
    "PP": ("psum", [128, W2], "float32"),
    "T1": ("psum", [128, W2], "float32"),
    "V7": ("psum", [128, W2], "float32"),
    "U": ("psum", [128, W2], "float32"),
}
SEMAPHORES = (["lda", "ldb", "ldm", "sent", "st", "mvb", "mvo", "mvm", "xc", "dv", "ac"]
              + ["rs%d" % j for j in range(NP)] + ["ag%d" % j for j in range(NP)])


def _plan(T, topo):
    cores = list(T.cores)
    n = len(cores)
    chip = [topo.chip(c) for c in cores]
    mate = [[q for q in range(n) if topo.mates(chip[r], chip[q])][0] for r in range(n)]
    lows = sorted(set(min(r, mate[r]) for r in range(n)))
    pair = [lows.index(min(r, mate[r])) for r in range(n)]
    peers = [[[q for q in range(n) if pair[q] == k and (q == r or topo.same_plane(chip[q], chip[r]))][0]
              for k in range(len(lows))] for r in range(n)]
    ha, hb = [], []
    for r in range(n):
        cand = [c for c in range(topo.CHIPS * topo.CORES_PER_CHIP)
                if topo.chip(c) == chip[r] and c not in cores and topo.may_write(c, cores[mate[r]])]
        same = [c for c in cand if topo.die(c) == topo.die(cores[r])]
        a = (same or cand)[0]
        rest = [c for c in cand if c != a]
        far = [c for c in rest if topo.die(c) != topo.die(cores[r])]
        ha.append(a)
        hb.append((far or rest)[0])
    return cores, mate, lows, pair, peers, ha, hb


def _engines(topo, src, dsts):
    m = -1
    for d in dsts:
        m &= topo.mask(src, d)
    return [b for b in range(m.bit_length()) if (m >> b) & 1]


def _bits(eng):
    m = 0
    for b in eng:
        m |= 1 << b
    return m


def _dst(topo, c):
    rid, pid, _ = topo.addr(c)
    return DstId(rid=rid, pnc=pid)


def _runs(starts, width):
    out = []
    for s in sorted(starts):
        if out and out[-1][1] == s:
            out[-1][1] = s + width
        else:
            out.append([s, s + width])
    return out


def _rank_core(g, r, T, topo, plan):
    cores, mate, lows, pair, peers, ha, hb = plan
    sem = T.sem
    k = pair[r]
    me = cores[r]
    hs = [ha[peers[r][kk]] for kk in range(NP)]
    eng = _engines(topo, me, hs)
    wide = _engines(topo, me, [ha[r], hb[r]])
    home = [e for e in wide if e not in eng]
    ne = len(eng)

    def col(kk):
        return F * lows[kk % NP]

    g.sync.dma_start(T.MVW[:, 0:F], T.m[:]).then_inc(sem.ldm, 16)
    g.scalar.dma_start(T.MVW[:, F:2 * F], T.v[:]).then_inc(sem.ldm, 16)
    g.sync.dma_start(T.MVW[:, 2 * F:3 * F], T.w[:]).then_inc(sem.ldm, 16)
    ra = _runs([col(k + d) for d in (1, 2, 3, 4)], W2)
    rb = _runs([col(k + d) for d in (5, 0)], W2)
    for a, b in ra:
        g.sync.dma_start(T.G[:, a:b], T.gr[:, a:b]).then_inc(sem.lda, 16)
    for a, b in rb:
        g.sync.dma_start(T.G[:, a:b], T.gr[:, a:b]).then_inc(sem.ldb, 16)

    g.wait_ge(sem.ldm, 48)
    g.remote_dma_fused([RemoteDMATransfer(dst_ids=[_dst(topo, ha[r]), _dst(topo, hb[r])], dma_engine_mask=_bits(wide),
                                          remote_sem=sem.mvo, srcs=[T.MVW[:]], dsts=[T.MVA[:], T.MVA[:]])],
                       local_sem=sem.sent)
    sent = len(wide)

    def piece(d, engs):
        kk = (k + d) % NP
        return RemoteDMATransfer(dst_ids=[_dst(topo, hs[kk])], dma_engine_mask=_bits(engs),
                                 remote_sem=sem["rs%d" % k],
                                 src=T.G[:, col(kk):col(kk) + W2], dst=T.L[:, W2 * k:W2 * k + W2])

    q = ne // 4
    g.wait_ge(sem.lda, 16 * len(ra))
    g.remote_dma_fused([piece(d, eng[q * (d - 1):q * d]) for d in (1, 2, 3, 4)], local_sem=sem.sent)
    g.wait_ge(sem.ldb, 16 * len(rb))
    g.remote_dma_fused([piece(5, eng), piece(0, home)], local_sem=sem.sent)
    sent += 4 * q + ne + len(home)

    stores = [0]

    def put(queue, ds):
        for d in ds:
            queue.wait_ge(sem["ag%d" % ((k - d) % NP)], len(home) if d == 0 else ne)
        for a, b in _runs([col(k - d) for d in ds], W2):
            queue.dma_start(T.y[:, a:b], T.Y[:, a:b]).then_inc(sem.st, 16)
            stores[0] += 1

    g.sync.wait_ge(sem.mvb, len(home))
    g.sync.dma_start(T.mo[:], T.MV[:, 0:F]).then_inc(sem.st, 16)
    g.scalar.wait_ge(sem.mvb, len(home))
    g.scalar.dma_start(T.vo[:], T.MV[:, F:W2]).then_inc(sem.st, 16)
    put(g.sync, G_FIRST)
    put(g.scalar, G_SECOND)
    put(g.sync, G_THIRD)
    g.wait_ge(sem.sent, sent)
    g.wait_ge(sem.st, 16 * (2 + stores[0]))


def _helper_core(g, r, first, T, topo, plan):
    cores, mate, lows, pair, peers, ha, hb = plan
    sem = T.sem
    V, A = g.vector, g.scalar
    k = pair[r]
    me = ha[r] if first else hb[r]
    twin = ha[mate[r]] if first else hb[mate[r]]
    ranks = [cores[peers[r][kk]] for kk in range(NP)]
    eng = _engines(topo, me, ranks + [ha[mate[r]], hb[mate[r]]])
    home = [e for e in _engines(topo, me, [cores[r]]) if e not in eng]
    ne = len(eng)
    n_in = len(_engines(topo, cores[r], [ha[r], hb[r]]))
    offm, homem = _bits(eng), _bits(home)
    own = slice(0, F) if r < mate[r] else slice(F, W2)
    oth = slice(F, W2) if r < mate[r] else slice(0, F)
    add, sub, mul = AluOpType.add, AluOpType.subtract, AluOpType.mult

    n = [0]

    def vec(call, *a):
        if n[0]:
            V.wait_ge(sem.dv, n[0])
        call(*a).then_inc(sem.dv, 1)
        n[0] += 1
        return n[0]

    m3 = T.M3 if first else T.T1

    def prep(buf, cols):
        vec(V.tensor_scalar, m3[:, cols], buf[:, 0:F], 3.0, None, mul)
        vec(V.tensor_scalar, T.V7[:, cols], buf[:, F:2 * F], 7.0, None, mul)
        vec(V.tensor_copy, T.WP[:, cols], buf[:, 2 * F:3 * F])

    def slot(j):
        return T.L[:, W2 * j:W2 * j + W2]

    V.wait_ge(sem.mvo, n_in)
    prep(T.MVA, own)
    n_p = 0
    if first:
        order = [(k - d) % NP for d in (0, 1, 2, 3, 4, 5)]
        count = [len(home)] + [ne // 4] * 4 + [ne]
        for j, c in zip(order[:2], count[:2]):
            V.wait_ge(sem["rs%d" % j], c)
        vec(V.tensor_tensor, T.ACC[:], slot(order[0]), slot(order[1]), add)
        for j, c in zip(order[2:5], count[2:5]):
            V.wait_ge(sem["rs%d" % j], c)
            vec(V.tensor_tensor, T.ACC[:], T.ACC[:], slot(j), add)
        V.wait_ge(sem["rs%d" % order[5]], count[5])
        n_p = vec(V.tensor_tensor, T.P[:], T.ACC[:], slot(order[5]), add)
        vec(V.tensor_copy, T.PP[:], T.P[:])
        V.wait_ge(sem.mvm, ne)
        prep(T.MVB, oth)
        vec(V.tensor_tensor, T.T1[:], T.P[:], T.M3[:], add)
        V.wait_ge(sem.xc, ne)
        n_s = vec(V.tensor_tensor, T.S[:], T.PP[:], T.PM[:], add)
        vec(V.tensor_tensor, T.T1[:], T.T1[:], T.PM[:], add)
    else:
        V.wait_ge(sem.mvm, ne)
        prep(T.MVB, oth)
        V.wait_ge(sem.xc, 2 * ne)
        n_s = vec(V.tensor_tensor, T.S[:], T.P[:], T.PM[:], add)
        vec(V.tensor_tensor, T.T1[:], T.T1[:], T.S[:], add)
    V.wait_ge(sem.ac, 1)
    n_v8 = vec(V.tensor_tensor, T.V8[:], T.V7[:], T.Q[:], add)
    n_mv = 0
    if first:
        vec(V.tensor_scalar, T.MVO[:, 0:F], T.T1[:, own], 0.25, None, mul)
        n_mv = vec(V.tensor_scalar, T.MVO[:, F:W2], T.V8[:, own], 0.125, None, mul)
    V.wait_ge(sem.ac, 2)
    vec(V.tensor_scalar, T.D[:], T.R2[:], 0.002, None, add)
    vec(V.reciprocal, T.I[:], T.D[:])
    vec(V.tensor_tensor, T.U[:], T.T1[:], T.I[:], mul)
    n_w = vec(V.tensor_tensor, T.WO[:], T.WP[:], T.U[:], sub)

    A.wait_ge(sem.dv, n_s)
    A.activation(T.Q[:], T.S[:], ActivationFunctionType.Square).then_inc(sem.ac, 1)
    A.wait_ge(sem.dv, n_v8)
    A.activation(T.R2[:], T.V8[:], ActivationFunctionType.Sqrt, scale=0.5).then_inc(sem.ac, 1)

    ycols = T.Y[:, F * lows[k]:F * lows[k] + W2]

    def cast(ds, mask):
        return RemoteDMATransfer(dst_ids=[_dst(topo, ranks[(k + d) % NP]) for d in ds], dma_engine_mask=mask,
                                 remote_sem=sem["ag%d" % k], srcs=[T.WO[:]], dsts=[ycols for d in ds])

    rid, pid, _ = topo.addr(twin)
    g.wait_ge(sem.mvo, n_in)
    g.remote_dma(out_ap=T.MVB[:], in_ap=T.MVA[:], remote_sem=sem.mvm, local_sem=sem.sent,
                 pid=pid, routing_id=rid, dma_engine_mask=offm)
    sent = ne
    if first:
        g.wait_ge(sem.dv, n_p)
        g.remote_dma_fused([RemoteDMATransfer(dst_ids=[_dst(topo, hb[mate[r]]), _dst(topo, hb[r]), _dst(topo, ha[mate[r]])],
                                              dma_engine_mask=offm, remote_sem=sem.xc,
                                              srcs=[T.P[:]], dsts=[T.PM[:], T.P[:], T.PM[:]])], local_sem=sem.sent)
        rid, pid, _ = topo.addr(cores[r])
        g.wait_ge(sem.dv, n_mv)
        g.remote_dma(out_ap=T.MV[:], in_ap=T.MVO[:], remote_sem=sem.mvb, local_sem=sem.sent,
                     pid=pid, routing_id=rid, dma_engine_mask=homem)
        g.wait_ge(sem.dv, n_w)
        g.remote_dma_fused([cast(D_A, offm), cast((0,), homem)], local_sem=sem.sent)
        sent += ne + len(home) + ne + len(home)
    else:
        g.wait_ge(sem.dv, n_w)
        g.remote_dma_fused([cast(D_B, offm)], local_sem=sem.sent)
        sent += ne
    g.wait_ge(sem.sent, sent)


def rank_program(g, core, T, topo):
    plan = _plan(T, topo)
    r = T.rank_of(core)
    if r is not None:
        _rank_core(g, r, T, topo, plan)
    elif core in plan[5]:
        _helper_core(g, plan[5].index(core), True, T, topo, plan)
    elif core in plan[6]:
        _helper_core(g, plan[6].index(core), False, T, topo, plan)
